import numpy as np
import ml_dtypes


def mxq(x, axis, fmt="e4m3"):
    dtype, down = {"e4m3": (ml_dtypes.float8_e4m3fn, 7), "e5m2": (ml_dtypes.float8_e5m2, 14)}[fmt]
    v = np.moveaxis(np.asarray(x, np.float32).astype(ml_dtypes.bfloat16).astype(np.float64), axis, -1)
    blocks = v.reshape(v.shape[:-1] + (-1, 32))
    amax = np.abs(blocks).max(-1, keepdims=True)
    byte = np.maximum(np.where(amax > 0, np.frexp(amax)[1] - 1 + 127, 0) - down, 1)
    scale = np.exp2(byte - 127.0)
    codes = (blocks / scale).astype(np.float32).astype(dtype).astype(np.float64)
    return np.moveaxis((codes * scale).reshape(v.shape), -1, axis)


WIDE = False


def mx_kscale(k):
    if not WIDE:
        return np.ones(k)
    levels = np.array([10, -10, 5, -5, 0])
    if k % 512:
        return np.exp2(np.random.permutation(np.resize(levels, k // 32))).repeat(32)
    a = np.empty((k // 512, 16))
    for p in range(k // 512):
        a[p, :8] = np.random.permutation(np.resize(levels, 8))
        for g in range(8):
            far = levels[np.abs(levels - a[p, g]) >= 10]
            a[p, g + 8] = far[np.random.randint(len(far))]
    return np.exp2(a.ravel()).repeat(32)


def f64(x):
    return np.asarray(x).astype(np.float64)


def striped(idx):
    return np.tile(idx.reshape(-1, 16).T, (8, 1)).astype(np.uint16)


def unstriped(offs):
    return offs[:16].T.reshape(-1).astype(np.int64)


def striped8(idx):
    return np.concatenate([x.reshape(-1, 16).T for x in idx]).astype(np.uint16)


def runs(offs, k):
    lists = np.stack([offs[16 * r : 16 * r + 16].T.reshape(-1) for r in range(8)]).astype(np.int64)
    return lists[np.arange(k) % 512 // 64]


def pack_weight(w):
    k, n = w.shape
    w = f64(np.asarray(w, np.float32).astype(ml_dtypes.bfloat16)).reshape(k // 32, 32, n)
    amax = np.abs(w).max(1)
    byte = np.clip(np.where(amax > 0, np.frexp(amax)[1] - 1 + 127 - 7, 1), 1, 254)
    scaled = (w * np.exp2(127.0 - byte)[:, None, :]).reshape(k, n).astype(np.float32)
    words = np.ascontiguousarray(scaled.reshape(k // 512, 128, 4, n).transpose(0, 1, 3, 2)).astype(ml_dtypes.float8_e4m3fn).view(np.uint8)
    return words, np.ascontiguousarray(byte.astype(np.uint8).reshape(k // 512, 16, n))


def unpack_weight(words, scales):
    g, p, n, _ = words.shape
    vals = np.ascontiguousarray(words).view(ml_dtypes.float8_e4m3fn).astype(np.float64) * np.repeat(np.exp2(scales.astype(np.float64) - 127.0), 8, axis=1)[..., None]
    return vals.transpose(0, 1, 3, 2).reshape(g * 512, n)

def planes(y):
    n, m = y.shape
    v = y.astype(np.float32).astype(ml_dtypes.bfloat16).astype(np.float64).reshape(n // 32, 32, m)
    top = np.abs(v).max(1)
    byte = np.clip(np.where(top > 0, np.frexp(top)[1] - 1 + 127 - 7, 1), 1, 254)
    codes = (v * np.exp2(127.0 - byte)[:, None, :]).reshape(n, m).astype(np.float32).astype(ml_dtypes.float8_e4m3fn).view(np.uint8)
    words = codes.reshape(n // 512, 128, 4, m).transpose(0, 1, 3, 2)
    return np.ascontiguousarray(words), np.ascontiguousarray(byte.astype(np.uint8).reshape(n // 512, 16, m))


K, T, S, G, H = 512, 2048, 512, 2048, 512


def setup_inputs():
    n = np.random.standard_normal
    s = mx_kscale(K)[:, None]
    packed_xT = pack_weight(n((K, T)) * s)
    packed_dT = pack_weight(n((K, G)) / s)
    return {
        "x_words": packed_xT[0],
        "x_scales": packed_xT[1],
        "d_words": packed_dT[0],
        "d_scales": packed_dT[1],
        "gs": (np.random.uniform(0.5, 1.5, (K, 1)) * s).astype(np.float32),
        "offs": striped(np.random.permutation(T)[:S]),
        "k1": striped8(np.random.randint(0, G, (8, H))),
        "n1": striped8(np.stack([np.random.permutation(S) for _ in range(8)])),
        "n2": striped8(np.stack([np.random.permutation(S) for _ in range(8)])),
        "n3": striped8(np.stack([np.random.permutation(S) for _ in range(8)])),
        "n4": striped8(np.stack([np.random.permutation(S) for _ in range(8)])),
    }


def reference(x_words, x_scales, d_words, d_scales, gs, offs, k1, n1, n2, n3, n4):
    d_k1 = unpack_weight(d_words, d_scales)[np.arange(K)[:, None], runs(k1, K)]
    xq = unpack_weight(x_words, x_scales)[:, unstriped(offs)]
    h = 0.0625 * (d_k1.T @ xq)
    z = f64(gs) * ((np.tanh(h[np.arange(H)[:, None], runs(n1, H)] - h)) * (h[np.arange(H)[:, None], runs(n2, H)]))
    h2 = 0.0625 * ((d_k1.T @ mxq(z, 0, "e4m3")))
    out_0 = h2[np.arange(H)[:, None], runs(n3, H)] - (h2[np.arange(H)[:, None], runs(n4, H)])
    return (out_0,) + planes(out_0)

@@ -1,0 +1,236 @@
+from contextlib import ExitStack
+
+import concourse.mybir as mybir
+
+F32 = mybir.dt.float32
+BF16 = mybir.dt.bfloat16
+I32 = mybir.dt.int32
+U32 = mybir.dt.uint32
+U16 = mybir.dt.uint16
+U8 = mybir.dt.uint8
+FP8X4 = mybir.dt.float8_e4m3fn_x4
+SUB = mybir.AluOpType.subtract
+MUL = mybir.AluOpType.mult
+COPY = mybir.ActivationFunctionType.Copy
+TANH = mybir.ActivationFunctionType.Tanh
+
+P = 128
+PACK = 4
+TABLE = 2048
+S = 512
+HALF = 256
+SIXTEENTH = 0.0625
+BIG = 2.0**127
+CHUNKS = ((0, 256), (256, 384), (384, 512))
+FLOPS = 2 * 2 * 512 * 512 * 512
+
+
+def entries(lst, a, b):
+    return lst[:, a // 16 : b // 16]
+
+
+def tile_picked_ringfdifgap_none_po_kernel(
+    tc, x_words, x_scales, d_words, d_scales, gs, offs, k1, n1, n2, n3, n4, out_0, out_1, out_2
+):
+    nc = tc.nc
+    with ExitStack() as ctx:
+        keep = ctx.enter_context(tc.tile_pool(name="keep", bufs=1))
+        psum = ctx.enter_context(tc.psum_pool(name="psum", bufs=8))
+
+        def sb(shape, dtype, name):
+            return keep.tile(shape, dtype, name=name, align_bytes=64)
+
+        def bank():
+            return psum.tile([P, S], F32, name="bank")
+
+        lists = {}
+
+        def load_list(name, src):
+            lists[name] = keep.tile([P, S // 16], U16, name="list_" + name)
+            nc.sync.dma_start(lists[name][:], src)
+
+        d_byte_table = sb([P, TABLE], U8, "d_byte_table")
+        x_byte_table = sb([P, TABLE], U8, "x_byte_table")
+        d_word_table = sb([P, TABLE], I32, "d_word_table")
+        x_word_table = sb([P, TABLE], I32, "x_word_table")
+        load_list("k1", k1)
+        nc.sync.dma_start(
+            d_byte_table[:].bitcast(I32), d_scales[0].bitcast(I32).unsqueeze(1).broadcast_to([16, 8, TABLE // 4])
+        )
+        load_list("offs", offs)
+        for q in range(4):
+            nc.sync.dma_start(
+                x_byte_table[:].bitcast(I32)[32 * q : 32 * q + 32, :],
+                x_scales[0].bitcast(I32)[4 * q : 4 * q + 4, :].unsqueeze(0).broadcast_to([8, 4, TABLE // 4]),
+            )
+        nc.sync.dma_start(d_word_table[:], d_words[0].rearrange("p n t -> p (n t)").bitcast(I32))
+        gain = sb([P, PACK], F32, "gain")
+        nc.sync.dma_start(gain[:], gs.rearrange("(p t) o -> p (t o)", t=PACK))
+        nc.sync.dma_start(x_word_table[:], x_words[0].rearrange("p n t -> p (n t)").bitcast(I32))
+        for name, src in (("n1", n1), ("n2", n2), ("n3", n3), ("n4", n4)):
+            load_list(name, src)
+
+        warm = sb([P, PACK], F32, "warm")
+        nc.scalar.activation(warm[:], gain[:], TANH)
+        gain16 = sb([P, PACK], F32, "gain16")
+        nc.scalar.activation(gain16[:], gain[:], COPY, scale=SIXTEENTH)
+
+        d_bytes_picked = sb([P, S], U8, "d_bytes_picked")
+        nc.vector.tensor_copy(d_bytes_picked[:], d_byte_table[:].indirect(lists["k1"][:]))
+        d_bytes = sb([P, S], U8, "d_bytes")
+        nc.vector.tensor_copy(
+            d_bytes[:].rearrange("p (t m) -> p t m", t=PACK), d_bytes_picked[:].rearrange("p (m t) -> p t m", t=PACK)
+        )
+        for r in range(1, 4):
+            nc.scalar.dma_start(d_bytes[:].bitcast(I32)[r:P:32, :], d_bytes[:].bitcast(I32)[8 * r : P : 32, :])
+
+        x_bytes = sb([P, S], U8, "x_bytes")
+        nc.vector.tensor_copy(x_bytes[:], x_byte_table[:].indirect(lists["offs"][:]))
+
+        d_words_picked = sb([P, S], U32, "d_words_picked")
+        nc.vector.tensor_copy(d_words_picked[:], d_word_table[:].bitcast(U32).indirect(lists["k1"][:]))
+        d_codes = sb([P, S], U32, "d_codes")
+        nc.vector.tensor_copy(
+            d_codes[:].rearrange("p (t m) -> p t m", t=PACK), d_words_picked[:].rearrange("p (m t) -> p t m", t=PACK)
+        )
+
+        x_codes = sb([P, S], U32, "x_codes")
+
+        def pick_x(a, b):
+            nc.vector.tensor_copy(x_codes[:, a:b], x_word_table[:].bitcast(U32).indirect(entries(lists["offs"], a, b)))
+
+        def product(dst, t, codes, scales, a, b):
+            nc.tensor.matmul_mx(
+                out=dst,
+                lhsT=d_codes[:, t * P : (t + 1) * P].bitcast(FP8X4),
+                lhsT_scale=d_bytes[:, t * P : (t + 1) * P],
+                rhs=codes[:, a:b].bitcast(FP8X4),
+                rhs_scale=scales[:, a:b],
+                start=True,
+                stop=True,
+            )
+
+        inverse = sb([P, PACK], F32, "inverse")
+        nc.vector.reciprocal(inverse[:], gain[:])
+        ungain = sb([P, PACK], F32, "ungain")
+        nc.vector.tensor_scalar(ungain[:], inverse[:], BIG, -BIG, mybir.AluOpType.min, mybir.AluOpType.max)
+
+        acc = {}
+        pick_x(0, HALF)
+        for t in (0, 1):
+            acc[t, 0] = bank()[:, 0:HALF]
+            product(acc[t, 0], t, x_codes, x_bytes, 0, HALF)
+        pick_x(HALF, S)
+        for t in (0, 1):
+            acc[t, 1] = bank()[:, 0:HALF]
+            product(acc[t, 1], t, x_codes, x_bytes, HALF, S)
+        for t in (2, 3):
+            acc[t] = bank()[:]
+            product(acc[t], t, x_codes, x_bytes, 0, S)
+
+        hw = [sb([P, S], F32, "hw%d" % t) for t in range(PACK)]
+        hp = [sb([P, S], F32, "hp%d" % t) for t in range(PACK)]
+        diff = [sb([P, S], F32, "diff%d" % t) for t in range(PACK)]
+        bend = [sb([P, S], F32, "bend%d" % t) for t in range(PACK)]
+        zf = [sb([P, PACK, b - a], F32, "zf%d" % a) for a, b in CHUNKS]
+        zb = [sb([P, b - a, PACK], BF16, "zb%d" % a) for a, b in CHUNKS]
+        z_codes = sb([P, S], U32, "z_codes")
+        z_bytes = sb([P, S], U8, "z_bytes")
+
+        def half(h):
+            return slice(h * HALF, (h + 1) * HALF)
+
+        def sub1(t, h):
+            nc.vector.tensor_tensor(
+                diff[t][:, half(h)], hw[t][:].indirect(entries(lists["n1"], h * HALF, (h + 1) * HALF)), hp[t][:, half(h)], SUB
+            )
+
+        def tanh(t, h):
+            nc.scalar.activation(bend[t][:, half(h)], diff[t][:, half(h)], TANH, scale=ungain[:, t : t + 1])
+
+        def mul2(t, c):
+            a, b = CHUNKS[c]
+            nc.vector.tensor_tensor(zf[c][:, t, :], hw[t][:].indirect(entries(lists["n2"], a, b)), bend[t][:, a:b], MUL)
+
+        def weave(copy, dst, src):
+            copy(dst[:].rearrange("p (c i) t -> p c t i", i=4), src[:].rearrange("p t (c i) -> p c t i", i=4))
+
+        def quantise(codes, scales, src, c):
+            a, b = CHUNKS[c]
+            nc.vector.quantize_mx(
+                out=codes[:, a:b].bitcast(FP8X4), scales=scales[:, a:b], in_=src[:].rearrange("p c t -> p (c t)")
+            )
+
+        def out_of(dst, src, scale):
+            nc.scalar.activation(dst, src, COPY, scale=scale)
+
+        for t in (0, 1):
+            out_of(hw[t][:, half(0)], acc[t, 0], gain16[:, t : t + 1])
+            nc.vector.tensor_scalar_mul(hp[t][:, half(0)], acc[t, 0], gain16[:, t : t + 1])
+        for t in (0, 1):
+            out_of(hw[t][:, half(1)], acc[t, 1], gain16[:, t : t + 1])
+            out_of(hp[t][:, half(1)], acc[t, 1], gain16[:, t : t + 1])
+            sub1(t, 0)
+            sub1(t, 1)
+        for t in (2, 3):
+            tanh(t - 2, 0)
+            mul2(t - 2, 0)
+            out_of(hw[t][:], acc[t], gain16[:, t : t + 1])
+            out_of(hp[t][:], acc[t], gain16[:, t : t + 1])
+            sub1(t, 0)
+            sub1(t, 1)
+        for t in (2, 3):
+            tanh(t, 0)
+            mul2(t, 0)
+        for t in range(PACK):
+            tanh(t, 1)
+            mul2(t, 1)
+        weave(nc.scalar.copy, zb[0], zf[0])
+        quantise(z_codes, z_bytes, zb[0], 0)
+        acc2 = [bank() for t in range(PACK)]
+        for t in range(PACK):
+            product(acc2[t][:, 0:256], t, z_codes, z_bytes, 0, 256)
+        for t in range(PACK):
+            mul2(t, 2)
+        weave(nc.scalar.copy, zb[1], zf[1])
+        quantise(z_codes, z_bytes, zb[1], 1)
+        for t in range(PACK):
+            product(acc2[t][:, 256:384], t, z_codes, z_bytes, 256, 384)
+        weave(nc.vector.tensor_copy, zb[2], zf[2])
+        quantise(z_codes, z_bytes, zb[2], 2)
+        last = [bank() for t in range(PACK)]
+        for t in range(PACK):
+            product(last[t][:, 0:128], t, z_codes, z_bytes, 384, 512)
+
+        h2 = [sb([P, S], F32, "h2_%d" % t) for t in range(PACK)]
+        g4 = [sb([P, S], F32, "g4_%d" % t) for t in range(PACK)]
+        of = [sb([P, PACK, b - a], F32, "of%d" % a) for a, b in CHUNKS]
+        ob = [sb([P, b - a, PACK], BF16, "ob%d" % a) for a, b in CHUNKS]
+        o_codes = sb([P, S], U32, "o_codes")
+        o_bytes = sb([P, S], U8, "o_bytes")
+        out_rows = out_0.rearrange("(p t) j -> p t j", t=PACK)
+        out_codes = out_1[0].rearrange("p c t -> p (c t)").bitcast(I32)
+
+        def sub3(t, c):
+            a, b = CHUNKS[c]
+            nc.vector.tensor_tensor(of[c][:, t, :], h2[t][:].indirect(entries(lists["n3"], a, b)), g4[t][:, a:b], SUB)
+
+        for t in range(PACK):
+            out_of(h2[t][:, 0:384], acc2[t][:, 0:384], SIXTEENTH)
+            out_of(h2[t][:, 384:512], last[t][:, 0:128], SIXTEENTH)
+            for h in (0, 1):
+                nc.vector.tensor_copy(g4[t][:, half(h)], h2[t][:].indirect(entries(lists["n4"], h * HALF, (h + 1) * HALF)))
+            if t > 0:
+                sub3(t - 1, 0)
+        sub3(PACK - 1, 0)
+        for c, (a, b) in enumerate(CHUNKS):
+            nc.sync.dma_start(out_rows[:, :, a:b], of[c][:])
+            weave(nc.scalar.copy if c < 2 else nc.vector.tensor_copy, ob[c], of[c])
+            if c < 2:
+                for t in range(PACK):
+                    sub3(t, c + 1)
+            quantise(o_codes, o_bytes, ob[c], c)
+            nc.sync.dma_start(out_codes[:, a:b], o_codes[:].bitcast(I32)[:, a:b])
+        for q in range(4):
+            queue = nc.sync if q < 2 else nc.scalar
+            queue.dma_start(out_2[0].bitcast(I32)[4 * q : 4 * q + 4, :], o_bytes[:].bitcast(I32)[32 * q : 32 * q + 4, :])

@@ -37,8 +37,8 @@ def tile_picked_ringfdifgap_none_po_kernel(
         keep = ctx.enter_context(tc.tile_pool(name="keep", bufs=1))
         psum = ctx.enter_context(tc.psum_pool(name="psum", bufs=8))
 
-        def sb(shape, dtype, name):
-            return keep.tile(shape, dtype, name=name, align_bytes=64)
+        def sb(shape, dtype, name, tag=None):
+            return keep.tile(shape, dtype, name=name, tag=tag or name, align_bytes=64)
 
         def bank():
             return psum.tile([P, S], F32, name="bank")
@@ -54,24 +54,26 @@ def tile_picked_ringfdifgap_none_po_kernel(
         d_word_table = sb([P, TABLE], I32, "d_word_table")
         x_word_table = sb([P, TABLE], I32, "x_word_table")
         load_list("k1", k1)
+        gain = sb([P, PACK], F32, "gain")
+        nc.gpsimd.dma_start(gain[:], gs.rearrange("(p t) o -> p (t o)", t=PACK))
         nc.sync.dma_start(
             d_byte_table[:].bitcast(I32), d_scales[0].bitcast(I32).unsqueeze(1).broadcast_to([16, 8, TABLE // 4])
         )
         load_list("offs", offs)
-        for q in range(4):
+        for q in (0, 2, 1, 3):
             nc.sync.dma_start(
                 x_byte_table[:].bitcast(I32)[32 * q : 32 * q + 32, :],
                 x_scales[0].bitcast(I32)[4 * q : 4 * q + 4, :].unsqueeze(0).broadcast_to([8, 4, TABLE // 4]),
             )
         nc.sync.dma_start(d_word_table[:], d_words[0].rearrange("p n t -> p (n t)").bitcast(I32))
-        gain = sb([P, PACK], F32, "gain")
-        nc.sync.dma_start(gain[:], gs.rearrange("(p t) o -> p (t o)", t=PACK))
         nc.sync.dma_start(x_word_table[:], x_words[0].rearrange("p n t -> p (n t)").bitcast(I32))
         for name, src in (("n1", n1), ("n2", n2), ("n3", n3), ("n4", n4)):
             load_list(name, src)
 
-        warm = sb([P, PACK], F32, "warm")
-        nc.scalar.activation(warm[:], gain[:], TANH)
+        cold = sb([P, 1], F32, "cold")
+        nc.gpsimd.memset(cold[:], 0.0)
+        warm = sb([P, 1], F32, "warm")
+        nc.scalar.activation(warm[:], cold[:], TANH)
         gain16 = sb([P, PACK], F32, "gain16")
         nc.scalar.activation(gain16[:], gain[:], COPY, scale=SIXTEENTH)
 
@@ -91,7 +93,7 @@ def tile_picked_ringfdifgap_none_po_kernel(
         nc.vector.tensor_copy(d_words_picked[:], d_word_table[:].bitcast(U32).indirect(lists["k1"][:]))
         d_codes = sb([P, S], U32, "d_codes")
         nc.vector.tensor_copy(
-            d_codes[:].rearrange("p (t m) -> p t m", t=PACK), d_words_picked[:].rearrange("p (m t) -> p t m", t=PACK)
+            d_codes[:].rearrange("p (t m) -> p m t", t=PACK), d_words_picked[:].rearrange("p (m t) -> p m t", t=PACK)
         )
 
         x_codes = sb([P, S], U32, "x_codes")
@@ -110,7 +112,7 @@ def tile_picked_ringfdifgap_none_po_kernel(
                 stop=True,
             )
 
-        inverse = sb([P, PACK], F32, "inverse")
+        inverse = sb([P, PACK], F32, "inverse", tag="d_words_picked")
         nc.vector.reciprocal(inverse[:], gain[:])
         ungain = sb([P, PACK], F32, "ungain")
         nc.vector.tensor_scalar(ungain[:], inverse[:], BIG, -BIG, mybir.AluOpType.min, mybir.AluOpType.max)
@@ -128,37 +130,38 @@ def tile_picked_ringfdifgap_none_po_kernel(
             acc[t] = bank()[:]
             product(acc[t], t, x_codes, x_bytes, 0, S)
 
-        hw = [sb([P, S], F32, "hw%d" % t) for t in range(PACK)]
-        hp = [sb([P, S], F32, "hp%d" % t) for t in range(PACK)]
+        wide = [sb([P, 2 * S], F32, "wide%d" % t) for t in range(1, PACK)]
+        first = sb([P, S], F32, "first")
+        plain_last = sb([P, S], F32, "plain_last")
+        window = [first[:]] + [w[:] for w in wide]
+        hw = [first[:]] + [w[:, 0:S] for w in wide]
+        hp = [w[:, S : 2 * S] for w in wide] + [plain_last[:]]
         diff = [sb([P, S], F32, "diff%d" % t) for t in range(PACK)]
         bend = [sb([P, S], F32, "bend%d" % t) for t in range(PACK)]
         zf = [sb([P, PACK, b - a], F32, "zf%d" % a) for a, b in CHUNKS]
-        zb = [sb([P, b - a, PACK], BF16, "zb%d" % a) for a, b in CHUNKS]
+        zb = [sb([P, HALF, PACK], BF16, "zb%d" % h) for h in range(2)]
         z_codes = sb([P, S], U32, "z_codes")
         z_bytes = sb([P, S], U8, "z_bytes")
 
         def half(h):
             return slice(h * HALF, (h + 1) * HALF)
 
-        def sub1(t, h):
-            nc.vector.tensor_tensor(
-                diff[t][:, half(h)], hw[t][:].indirect(entries(lists["n1"], h * HALF, (h + 1) * HALF)), hp[t][:, half(h)], SUB
-            )
+        def sub1(t, a, b):
+            nc.vector.tensor_tensor(diff[t][:, a:b], window[t].indirect(entries(lists["n1"], a, b)), hp[t][:, a:b], SUB)
 
-        def tanh(t, h):
-            nc.scalar.activation(bend[t][:, half(h)], diff[t][:, half(h)], TANH, scale=ungain[:, t : t + 1])
+        def tanh(t, a, b):
+            nc.scalar.activation(bend[t][:, a:b], diff[t][:, a:b], TANH, scale=ungain[:, t : t + 1])
 
         def mul2(t, c):
             a, b = CHUNKS[c]
-            nc.vector.tensor_tensor(zf[c][:, t, :], hw[t][:].indirect(entries(lists["n2"], a, b)), bend[t][:, a:b], MUL)
+            nc.vector.tensor_tensor(zf[c][:, t, :], window[t].indirect(entries(lists["n2"], a, b)), bend[t][:, a:b], MUL)
 
         def weave(copy, dst, src):
-            copy(dst[:].rearrange("p (c i) t -> p c t i", i=4), src[:].rearrange("p t (c i) -> p c t i", i=4))
+            copy(dst.rearrange("p (c i) t -> p c t i", i=4), src[:].rearrange("p t (c i) -> p c t i", i=4))
 
-        def quantise(codes, scales, src, c):
-            a, b = CHUNKS[c]
+        def quantise(codes, scales, src, h):
             nc.vector.quantize_mx(
-                out=codes[:, a:b].bitcast(FP8X4), scales=scales[:, a:b], in_=src[:].rearrange("p c t -> p (c t)")
+                out=codes[:, half(h)].bitcast(FP8X4), scales=scales[:, half(h)], in_=src[:].rearrange("p c t -> p (c t)")
             )
 
         def out_of(dst, src, scale):
@@ -170,42 +173,41 @@ def tile_picked_ringfdifgap_none_po_kernel(
         for t in (0, 1):
             out_of(hw[t][:, half(1)], acc[t, 1], gain16[:, t : t + 1])
             out_of(hp[t][:, half(1)], acc[t, 1], gain16[:, t : t + 1])
-            sub1(t, 0)
-            sub1(t, 1)
+        sub1(0, 0, HALF)
+        sub1(0, HALF, S)
+        sub1(1, 0, S)
         for t in (2, 3):
-            tanh(t - 2, 0)
+            tanh(t - 2, 0, HALF)
             mul2(t - 2, 0)
-            out_of(hw[t][:], acc[t], gain16[:, t : t + 1])
-            out_of(hp[t][:], acc[t], gain16[:, t : t + 1])
-            sub1(t, 0)
-            sub1(t, 1)
+            out_of(hw[t], acc[t], gain16[:, t : t + 1])
+            out_of(hp[t], acc[t], gain16[:, t : t + 1])
+            sub1(t, 0, S)
         for t in (2, 3):
-            tanh(t, 0)
+            tanh(t, 0, HALF)
             mul2(t, 0)
         for t in range(PACK):
-            tanh(t, 1)
+            tanh(t, *CHUNKS[1])
             mul2(t, 1)
-        weave(nc.scalar.copy, zb[0], zf[0])
+        weave(nc.scalar.copy, zb[0][:], zf[0])
         quantise(z_codes, z_bytes, zb[0], 0)
-        acc2 = [bank() for t in range(PACK)]
+        acc2 = {}
         for t in range(PACK):
-            product(acc2[t][:, 0:256], t, z_codes, z_bytes, 0, 256)
+            acc2[t, 0] = bank()[:, 0:HALF]
+            product(acc2[t, 0], t, z_codes, z_bytes, 0, HALF)
         for t in range(PACK):
+            tanh(t, *CHUNKS[2])
             mul2(t, 2)
-        weave(nc.scalar.copy, zb[1], zf[1])
+        weave(nc.scalar.copy, zb[1][:, 0:128, :], zf[1])
+        weave(nc.vector.tensor_copy, zb[1][:, 128:256, :], zf[2])
         quantise(z_codes, z_bytes, zb[1], 1)
         for t in range(PACK):
-            product(acc2[t][:, 256:384], t, z_codes, z_bytes, 256, 384)
-        weave(nc.vector.tensor_copy, zb[2], zf[2])
-        quantise(z_codes, z_bytes, zb[2], 2)
-        last = [bank() for t in range(PACK)]
-        for t in range(PACK):
-            product(last[t][:, 0:128], t, z_codes, z_bytes, 384, 512)
+            acc2[t, 1] = bank()[:, 0:HALF]
+            product(acc2[t, 1], t, z_codes, z_bytes, HALF, S)
 
         h2 = [sb([P, S], F32, "h2_%d" % t) for t in range(PACK)]
         g4 = [sb([P, S], F32, "g4_%d" % t) for t in range(PACK)]
         of = [sb([P, PACK, b - a], F32, "of%d" % a) for a, b in CHUNKS]
-        ob = [sb([P, b - a, PACK], BF16, "ob%d" % a) for a, b in CHUNKS]
+        ob = [sb([P, HALF, PACK], BF16, "ob%d" % h) for h in range(2)]
         o_codes = sb([P, S], U32, "o_codes")
         o_bytes = sb([P, S], U8, "o_bytes")
         out_rows = out_0.rearrange("(p t) j -> p t j", t=PACK)
@@ -216,21 +218,23 @@ def tile_picked_ringfdifgap_none_po_kernel(
             nc.vector.tensor_tensor(of[c][:, t, :], h2[t][:].indirect(entries(lists["n3"], a, b)), g4[t][:, a:b], SUB)
 
         for t in range(PACK):
-            out_of(h2[t][:, 0:384], acc2[t][:, 0:384], SIXTEENTH)
-            out_of(h2[t][:, 384:512], last[t][:, 0:128], SIXTEENTH)
+            for h in (0, 1):
+                out_of(h2[t][:, half(h)], acc2[t, h], SIXTEENTH)
             for h in (0, 1):
                 nc.vector.tensor_copy(g4[t][:, half(h)], h2[t][:].indirect(entries(lists["n4"], h * HALF, (h + 1) * HALF)))
             if t > 0:
                 sub3(t - 1, 0)
         sub3(PACK - 1, 0)
+        woven = ((nc.scalar.copy, ob[0][:]), (nc.scalar.copy, ob[1][:, 0:128, :]), (nc.vector.tensor_copy, ob[1][:, 128:256, :]))
         for c, (a, b) in enumerate(CHUNKS):
             nc.sync.dma_start(out_rows[:, :, a:b], of[c][:])
-            weave(nc.scalar.copy if c < 2 else nc.vector.tensor_copy, ob[c], of[c])
+            weave(woven[c][0], woven[c][1], of[c])
             if c < 2:
                 for t in range(PACK):
                     sub3(t, c + 1)
-            quantise(o_codes, o_bytes, ob[c], c)
-            nc.sync.dma_start(out_codes[:, a:b], o_codes[:].bitcast(I32)[:, a:b])
+        for h in (0, 1):
+            quantise(o_codes, o_bytes, ob[h], h)
+            nc.sync.dma_start(out_codes[:, half(h)], o_codes[:].bitcast(I32)[:, half(h)])
         for q in range(4):
             queue = nc.sync if q < 2 else nc.scalar
             queue.dma_start(out_2[0].bitcast(I32)[4 * q : 4 * q + 4, :], o_bytes[:].bitcast(I32)[32 * q : 32 * q + 4, :])

@@ -112,11 +112,6 @@ def tile_picked_ringfdifgap_none_po_kernel(
                 stop=True,
             )
 
-        inverse = sb([P, PACK], F32, "inverse", tag="d_words_picked")
-        nc.vector.reciprocal(inverse[:], gain[:])
-        ungain = sb([P, PACK], F32, "ungain")
-        nc.vector.tensor_scalar(ungain[:], inverse[:], BIG, -BIG, mybir.AluOpType.min, mybir.AluOpType.max)
-
         acc = {}
         pick_x(0, HALF)
         for t in (0, 1):
@@ -126,6 +121,10 @@ def tile_picked_ringfdifgap_none_po_kernel(
         for t in (0, 1):
             acc[t, 1] = bank()[:, 0:HALF]
             product(acc[t, 1], t, x_codes, x_bytes, HALF, S)
+        inverse = sb([P, PACK], F32, "inverse", tag="x_word_table")
+        nc.vector.reciprocal(inverse[:], gain[:])
+        ungain = sb([P, PACK], F32, "ungain")
+        nc.vector.tensor_scalar(ungain[:], inverse[:], BIG, -BIG, mybir.AluOpType.min, mybir.AluOpType.max)
         for t in (2, 3):
             acc[t] = bank()[:]
             product(acc[t], t, x_codes, x_bytes, 0, S)
@@ -139,7 +138,7 @@ def tile_picked_ringfdifgap_none_po_kernel(
         diff = [sb([P, S], F32, "diff%d" % t) for t in range(PACK)]
         bend = [sb([P, S], F32, "bend%d" % t) for t in range(PACK)]
         zf = [sb([P, PACK, b - a], F32, "zf%d" % a) for a, b in CHUNKS]
-        zb = [sb([P, HALF, PACK], BF16, "zb%d" % h) for h in range(2)]
+        zb = [sb([P, b - a, PACK], BF16, "zb%d" % a) for a, b in CHUNKS]
         z_codes = sb([P, S], U32, "z_codes")
         z_bytes = sb([P, S], U8, "z_bytes")
 
@@ -157,11 +156,16 @@ def tile_picked_ringfdifgap_none_po_kernel(
             nc.vector.tensor_tensor(zf[c][:, t, :], window[t].indirect(entries(lists["n2"], a, b)), bend[t][:, a:b], MUL)
 
         def weave(copy, dst, src):
-            copy(dst.rearrange("p (c i) t -> p c t i", i=4), src[:].rearrange("p t (c i) -> p c t i", i=4))
+            copy(dst.rearrange("p (c i) t -> p c t i", i=4), src.rearrange("p t (c i) -> p c t i", i=4))
 
-        def quantise(codes, scales, src, h):
+        def weave_last(dst, src):
+            weave(nc.vector.tensor_copy, dst[:, 0:64, :], src[:, :, 0:64])
+            weave(nc.scalar.copy, dst[:, 64:128, :], src[:, :, 64:128])
+
+        def quantise(codes, scales, src, c):
+            a, b = CHUNKS[c]
             nc.vector.quantize_mx(
-                out=codes[:, half(h)].bitcast(FP8X4), scales=scales[:, half(h)], in_=src[:].rearrange("p c t -> p (c t)")
+                out=codes[:, a:b].bitcast(FP8X4), scales=scales[:, a:b], in_=src[c][:].rearrange("p c t -> p (c t)")
             )
 
         def out_of(dst, src, scale):
@@ -186,28 +190,35 @@ def tile_picked_ringfdifgap_none_po_kernel(
             tanh(t, 0, HALF)
             mul2(t, 0)
         for t in range(PACK):
-            tanh(t, *CHUNKS[1])
+            tanh(t, HALF, S if t < 2 else CHUNKS[1][1])
             mul2(t, 1)
-        weave(nc.scalar.copy, zb[0][:], zf[0])
-        quantise(z_codes, z_bytes, zb[0], 0)
-        acc2 = {}
-        for t in range(PACK):
-            acc2[t, 0] = bank()[:, 0:HALF]
-            product(acc2[t, 0], t, z_codes, z_bytes, 0, HALF)
-        for t in range(PACK):
+        for t in (0, 1):
+            mul2(t, 2)
+        h2 = [sb([P, S], F32, "h2_%d" % t) for t in range(PACK)]
+
+        def second(t, a, b):
+            dst = bank()[:, 0 : b - a]
+            product(dst, t, z_codes, z_bytes, a, b)
+            return dst
+
+        weave(nc.scalar.copy, zb[0][:], zf[0][:])
+        quantise(z_codes, z_bytes, zb, 0)
+        early = [second(t, 0, HALF) for t in range(PACK)]
+        for t in (2, 3):
             tanh(t, *CHUNKS[2])
             mul2(t, 2)
-        weave(nc.scalar.copy, zb[1][:, 0:128, :], zf[1])
-        weave(nc.vector.tensor_copy, zb[1][:, 128:256, :], zf[2])
-        quantise(z_codes, z_bytes, zb[1], 1)
-        for t in range(PACK):
-            acc2[t, 1] = bank()[:, 0:HALF]
-            product(acc2[t, 1], t, z_codes, z_bytes, HALF, S)
+        weave(nc.scalar.copy, zb[1][:], zf[1][:])
+        out_of(h2[0][:, 0:HALF], early[0], SIXTEENTH)
+        weave_last(zb[2], zf[2])
+        for c in (1, 2):
+            quantise(z_codes, z_bytes, zb, c)
+            a, b = CHUNKS[c]
+            out_of(h2[0][:, a:b], second(0, a, b), SIXTEENTH)
+        late = [None] + [second(t, HALF, S) for t in range(1, PACK)]
 
-        h2 = [sb([P, S], F32, "h2_%d" % t) for t in range(PACK)]
         g4 = [sb([P, S], F32, "g4_%d" % t) for t in range(PACK)]
         of = [sb([P, PACK, b - a], F32, "of%d" % a) for a, b in CHUNKS]
-        ob = [sb([P, HALF, PACK], BF16, "ob%d" % h) for h in range(2)]
+        ob = [sb([P, b - a, PACK], BF16, "ob%d" % a) for a, b in CHUNKS]
         o_codes = sb([P, S], U32, "o_codes")
         o_bytes = sb([P, S], U8, "o_bytes")
         out_rows = out_0.rearrange("(p t) j -> p t j", t=PACK)
@@ -218,23 +229,25 @@ def tile_picked_ringfdifgap_none_po_kernel(
             nc.vector.tensor_tensor(of[c][:, t, :], h2[t][:].indirect(entries(lists["n3"], a, b)), g4[t][:, a:b], SUB)
 
         for t in range(PACK):
-            for h in (0, 1):
-                out_of(h2[t][:, half(h)], acc2[t, h], SIXTEENTH)
+            if t > 0:
+                out_of(h2[t][:, half(0)], early[t], SIXTEENTH)
+                out_of(h2[t][:, half(1)], late[t], SIXTEENTH)
             for h in (0, 1):
                 nc.vector.tensor_copy(g4[t][:, half(h)], h2[t][:].indirect(entries(lists["n4"], h * HALF, (h + 1) * HALF)))
             if t > 0:
                 sub3(t - 1, 0)
         sub3(PACK - 1, 0)
-        woven = ((nc.scalar.copy, ob[0][:]), (nc.scalar.copy, ob[1][:, 0:128, :]), (nc.vector.tensor_copy, ob[1][:, 128:256, :]))
         for c, (a, b) in enumerate(CHUNKS):
             nc.sync.dma_start(out_rows[:, :, a:b], of[c][:])
-            weave(woven[c][0], woven[c][1], of[c])
             if c < 2:
+                weave(nc.scalar.copy, ob[c][:], of[c][:])
                 for t in range(PACK):
                     sub3(t, c + 1)
-        for h in (0, 1):
-            quantise(o_codes, o_bytes, ob[h], h)
-            nc.sync.dma_start(out_codes[:, half(h)], o_codes[:].bitcast(I32)[:, half(h)])
+            else:
+                weave_last(ob[c], of[c])
+        for c, (a, b) in enumerate(CHUNKS):
+            quantise(o_codes, o_bytes, ob, c)
+            nc.sync.dma_start(out_codes[:, a:b], o_codes[:].bitcast(I32)[:, a:b])
         for q in range(4):
             queue = nc.sync if q < 2 else nc.scalar
             queue.dma_start(out_2[0].bitcast(I32)[4 * q : 4 * q + 4, :], o_bytes[:].bitcast(I32)[32 * q : 32 * q + 4, :])

@@ -93,7 +93,8 @@ def tile_picked_ringfdifgap_none_po_kernel(
         nc.vector.tensor_copy(d_words_picked[:], d_word_table[:].bitcast(U32).indirect(lists["k1"][:]))
         d_codes = sb([P, S], U32, "d_codes")
         nc.vector.tensor_copy(
-            d_codes[:].rearrange("p (t m) -> p m t", t=PACK), d_words_picked[:].rearrange("p (m t) -> p m t", t=PACK)
+            d_codes[:].rearrange("p (t m i) -> p m t i", t=PACK, i=4),
+            d_words_picked[:].rearrange("p (m i t) -> p m t i", t=PACK, i=4),
         )
 
         x_codes = sb([P, S], U32, "x_codes")
@@ -156,7 +157,7 @@ def tile_picked_ringfdifgap_none_po_kernel(
             nc.vector.tensor_tensor(zf[c][:, t, :], window[t].indirect(entries(lists["n2"], a, b)), bend[t][:, a:b], MUL)
 
         def weave(copy, dst, src):
-            copy(dst.rearrange("p (c i) t -> p c t i", i=4), src.rearrange("p t (c i) -> p c t i", i=4))
+            copy(dst.rearrange("p (c i) t -> p c t i", i=2), src.rearrange("p t (c i) -> p c t i", i=2))
 
         def weave_last(dst, src):
             weave(nc.vector.tensor_copy, dst[:, 0:64, :], src[:, :, 0:64])

@@ -9,246 +9,239 @@ U32 = mybir.dt.uint32
 U16 = mybir.dt.uint16
 U8 = mybir.dt.uint8
 FP8X4 = mybir.dt.float8_e4m3fn_x4
-SUB = mybir.AluOpType.subtract
-MUL = mybir.AluOpType.mult
+ALU = mybir.AluOpType
 COPY = mybir.ActivationFunctionType.Copy
 TANH = mybir.ActivationFunctionType.Tanh
 
 P = 128
 PACK = 4
+QUADRANT = 32
+SCALE_ROWS = 16
+REPEAT = P // SCALE_ROWS
+GROUP = 16
 TABLE = 2048
 S = 512
-HALF = 256
+HALF = S // 2
 SIXTEENTH = 0.0625
-BIG = 2.0**127
-CHUNKS = ((0, 256), (256, 384), (384, 512))
+LARGEST = 2.0**127
+VECTOR_SHARE = 160
+BANKS = 8
 FLOPS = 2 * 2 * 512 * 512 * 512
 
 
-def entries(lst, a, b):
-    return lst[:, a // 16 : b // 16]
+def half(h):
+    return slice(h * HALF, (h + 1) * HALF)
+
+
+def entries(offsets, cols):
+    return offsets[:, cols.start // GROUP : cols.stop // GROUP]
 
 
 def tile_picked_ringfdifgap_none_po_kernel(
     tc, x_words, x_scales, d_words, d_scales, gs, offs, k1, n1, n2, n3, n4, out_0, out_1, out_2
 ):
     nc = tc.nc
+    whole = slice(0, S)
     with ExitStack() as ctx:
         keep = ctx.enter_context(tc.tile_pool(name="keep", bufs=1))
-        psum = ctx.enter_context(tc.psum_pool(name="psum", bufs=8))
+        psum = ctx.enter_context(tc.psum_pool(name="psum", bufs=BANKS))
 
-        def sb(shape, dtype, name, tag=None):
+        def sbuf(shape, dtype, name, tag=None):
             return keep.tile(shape, dtype, name=name, tag=tag or name, align_bytes=64)
-
-        def bank():
-            return psum.tile([P, S], F32, name="bank")
 
         lists = {}
 
-        def load_list(name, src):
-            lists[name] = keep.tile([P, S // 16], U16, name="list_" + name)
-            nc.sync.dma_start(lists[name][:], src)
+        def load_list(name, source):
+            lists[name] = keep.tile([P, S // GROUP], U16, name="list_" + name)
+            nc.sync.dma_start(lists[name][:], source)
 
-        d_byte_table = sb([P, TABLE], U8, "d_byte_table")
-        x_byte_table = sb([P, TABLE], U8, "x_byte_table")
-        d_word_table = sb([P, TABLE], I32, "d_word_table")
-        x_word_table = sb([P, TABLE], I32, "x_word_table")
+        d_byte_table = sbuf([P, TABLE], U8, "d_byte_table")
+        x_byte_table = sbuf([P, TABLE], U8, "x_byte_table")
+        d_word_table = sbuf([P, TABLE], I32, "d_word_table")
+        x_word_table = sbuf([P, TABLE], I32, "x_word_table")
         load_list("k1", k1)
-        gain = sb([P, PACK], F32, "gain")
+        gain = sbuf([P, PACK], F32, "gain")
         nc.gpsimd.dma_start(gain[:], gs.rearrange("(p t) o -> p (t o)", t=PACK))
         nc.sync.dma_start(
-            d_byte_table[:].bitcast(I32), d_scales[0].bitcast(I32).unsqueeze(1).broadcast_to([16, 8, TABLE // 4])
+            d_byte_table[:].bitcast(I32),
+            d_scales[0].bitcast(I32).unsqueeze(1).broadcast_to([SCALE_ROWS, REPEAT, TABLE // 4]),
         )
         load_list("offs", offs)
         for q in (0, 2, 1, 3):
             nc.sync.dma_start(
-                x_byte_table[:].bitcast(I32)[32 * q : 32 * q + 32, :],
-                x_scales[0].bitcast(I32)[4 * q : 4 * q + 4, :].unsqueeze(0).broadcast_to([8, 4, TABLE // 4]),
+                x_byte_table[:].bitcast(I32)[QUADRANT * q : QUADRANT * (q + 1), :],
+                x_scales[0].bitcast(I32)[4 * q : 4 * q + 4, :].unsqueeze(0).broadcast_to([REPEAT, 4, TABLE // 4]),
             )
         nc.sync.dma_start(d_word_table[:], d_words[0].rearrange("p n t -> p (n t)").bitcast(I32))
         nc.sync.dma_start(x_word_table[:], x_words[0].rearrange("p n t -> p (n t)").bitcast(I32))
-        for name, src in (("n1", n1), ("n2", n2), ("n3", n3), ("n4", n4)):
-            load_list(name, src)
+        for name, source in (("n1", n1), ("n2", n2), ("n3", n3), ("n4", n4)):
+            load_list(name, source)
 
-        cold = sb([P, 1], F32, "cold")
-        nc.gpsimd.memset(cold[:], 0.0)
-        warm = sb([P, 1], F32, "warm")
-        nc.scalar.activation(warm[:], cold[:], TANH)
-        gain16 = sb([P, PACK], F32, "gain16")
+        gain16 = sbuf([P, PACK], F32, "gain16")
         nc.scalar.activation(gain16[:], gain[:], COPY, scale=SIXTEENTH)
 
-        d_bytes_picked = sb([P, S], U8, "d_bytes_picked")
+        d_bytes_picked = sbuf([P, S], U8, "d_bytes_picked")
         nc.vector.tensor_copy(d_bytes_picked[:], d_byte_table[:].indirect(lists["k1"][:]))
-        d_bytes = sb([P, S], U8, "d_bytes")
+        d_bytes = sbuf([P, S], U8, "d_bytes")
         nc.vector.tensor_copy(
             d_bytes[:].rearrange("p (t m) -> p t m", t=PACK), d_bytes_picked[:].rearrange("p (m t) -> p t m", t=PACK)
         )
         for r in range(1, 4):
-            nc.scalar.dma_start(d_bytes[:].bitcast(I32)[r:P:32, :], d_bytes[:].bitcast(I32)[8 * r : P : 32, :])
+            nc.scalar.dma_start(
+                d_bytes[:].bitcast(I32)[r:P:QUADRANT, :], d_bytes[:].bitcast(I32)[REPEAT * r : P : QUADRANT, :]
+            )
 
-        x_bytes = sb([P, S], U8, "x_bytes")
+        x_bytes = sbuf([P, S], U8, "x_bytes")
         nc.vector.tensor_copy(x_bytes[:], x_byte_table[:].indirect(lists["offs"][:]))
 
-        d_words_picked = sb([P, S], U32, "d_words_picked")
+        d_words_picked = sbuf([P, S], U32, "d_words_picked")
         nc.vector.tensor_copy(d_words_picked[:], d_word_table[:].bitcast(U32).indirect(lists["k1"][:]))
-        d_codes = sb([P, S], U32, "d_codes")
+        d_codes = sbuf([P, S], U32, "d_codes")
         nc.vector.tensor_copy(
             d_codes[:].rearrange("p (t m i) -> p m t i", t=PACK, i=4),
             d_words_picked[:].rearrange("p (m i t) -> p m t i", t=PACK, i=4),
         )
 
-        x_codes = sb([P, S], U32, "x_codes")
-
-        def pick_x(a, b):
-            nc.vector.tensor_copy(x_codes[:, a:b], x_word_table[:].bitcast(U32).indirect(entries(lists["offs"], a, b)))
-
-        def product(dst, t, codes, scales, a, b):
+        def product(t, codes, scales, cols):
+            bank = psum.tile([P, S], F32, name="bank")
+            sums = bank[:, 0 : cols.stop - cols.start]
             nc.tensor.matmul_mx(
-                out=dst,
+                out=sums,
                 lhsT=d_codes[:, t * P : (t + 1) * P].bitcast(FP8X4),
                 lhsT_scale=d_bytes[:, t * P : (t + 1) * P],
-                rhs=codes[:, a:b].bitcast(FP8X4),
-                rhs_scale=scales[:, a:b],
+                rhs=codes[:, cols].bitcast(FP8X4),
+                rhs_scale=scales[:, cols],
                 start=True,
                 stop=True,
             )
+            return sums
 
-        acc = {}
-        pick_x(0, HALF)
-        for t in (0, 1):
-            acc[t, 0] = bank()[:, 0:HALF]
-            product(acc[t, 0], t, x_codes, x_bytes, 0, HALF)
-        pick_x(HALF, S)
-        for t in (0, 1):
-            acc[t, 1] = bank()[:, 0:HALF]
-            product(acc[t, 1], t, x_codes, x_bytes, HALF, S)
-        inverse = sb([P, PACK], F32, "inverse", tag="x_word_table")
+        x_codes = sbuf([P, S], U32, "x_codes")
+        h_sums = {}
+        for h in (0, 1):
+            nc.vector.tensor_copy(
+                x_codes[:, half(h)], x_word_table[:].bitcast(U32).indirect(entries(lists["offs"], half(h)))
+            )
+            for t in (0, 1):
+                h_sums[t, h] = product(t, x_codes, x_bytes, half(h))
+        inverse = sbuf([P, PACK], F32, "inverse", tag="x_word_table")
         nc.vector.reciprocal(inverse[:], gain[:])
-        ungain = sb([P, PACK], F32, "ungain")
-        nc.vector.tensor_scalar(ungain[:], inverse[:], BIG, -BIG, mybir.AluOpType.min, mybir.AluOpType.max)
+        ungain = sbuf([P, PACK], F32, "ungain")
+        nc.vector.tensor_scalar(ungain[:], inverse[:], LARGEST, -LARGEST, ALU.min, ALU.max)
         for t in (2, 3):
-            acc[t] = bank()[:]
-            product(acc[t], t, x_codes, x_bytes, 0, S)
+            h_sums[t] = product(t, x_codes, x_bytes, whole)
 
-        wide = [sb([P, 2 * S], F32, "wide%d" % t) for t in range(1, PACK)]
-        first = sb([P, S], F32, "first")
-        plain_last = sb([P, S], F32, "plain_last")
-        window = [first[:]] + [w[:] for w in wide]
-        hw = [first[:]] + [w[:, 0:S] for w in wide]
-        hp = [w[:, S : 2 * S] for w in wide] + [plain_last[:]]
-        diff = [sb([P, S], F32, "diff%d" % t) for t in range(PACK)]
-        bend = [sb([P, S], F32, "bend%d" % t) for t in range(PACK)]
-        zf = [sb([P, PACK, b - a], F32, "zf%d" % a) for a, b in CHUNKS]
-        zb = [sb([P, b - a, PACK], BF16, "zb%d" % a) for a, b in CHUNKS]
-        z_codes = sb([P, S], U32, "z_codes")
-        z_bytes = sb([P, S], U8, "z_bytes")
+        window = [sbuf([P, 2 * S], F32, "window%d" % t) for t in range(PACK)]
+        nc.vector.memset(window[0][:, S : 2 * S], 0.0)
+        plain_last = sbuf([P, S], F32, "plain_last")
+        looked_up = [w[:, 0:S] for w in window]
+        plain = [w[:, S : 2 * S] for w in window[1:]] + [plain_last[:]]
+        diff = [sbuf([P, S], F32, "diff%d" % t) for t in range(PACK)]
+        tanh_diff = [sbuf([P, S], F32, "tanh_diff%d" % t) for t in range(PACK)]
+        z_f32 = [sbuf([P, PACK, HALF], F32, "z_f32_%d" % h) for h in (0, 1)]
+        z_bf16 = [sbuf([P, HALF, PACK], BF16, "z_bf16_%d" % h) for h in (0, 1)]
+        z_codes = sbuf([P, S], U32, "z_codes")
+        z_bytes = sbuf([P, S], U8, "z_bytes")
 
-        def half(h):
-            return slice(h * HALF, (h + 1) * HALF)
+        def leave_psum(dst, sums, scale):
+            nc.scalar.activation(dst, sums, COPY, scale=scale)
 
-        def sub1(t, a, b):
-            nc.vector.tensor_tensor(diff[t][:, a:b], window[t].indirect(entries(lists["n1"], a, b)), hp[t][:, a:b], SUB)
+        def difference(t, cols):
+            nc.vector.tensor_tensor(
+                diff[t][:, cols], window[t][:].indirect(entries(lists["n1"], cols)), plain[t][:, cols], ALU.subtract
+            )
 
-        def tanh(t, a, b):
-            nc.scalar.activation(bend[t][:, a:b], diff[t][:, a:b], TANH, scale=ungain[:, t : t + 1])
+        def tanh(t, h):
+            nc.scalar.activation(tanh_diff[t][:, half(h)], diff[t][:, half(h)], TANH, scale=ungain[:, t : t + 1])
 
-        def mul2(t, c):
-            a, b = CHUNKS[c]
-            nc.vector.tensor_tensor(zf[c][:, t, :], window[t].indirect(entries(lists["n2"], a, b)), bend[t][:, a:b], MUL)
+        def z_values(t, h):
+            nc.vector.tensor_tensor(
+                z_f32[h][:, t, :], window[t][:].indirect(entries(lists["n2"], half(h))), tanh_diff[t][:, half(h)], ALU.mult
+            )
 
         def weave(copy, dst, src):
             copy(dst.rearrange("p (c i) t -> p c t i", i=2), src.rearrange("p t (c i) -> p c t i", i=2))
 
-        def weave_last(dst, src):
-            weave(nc.vector.tensor_copy, dst[:, 0:64, :], src[:, :, 0:64])
-            weave(nc.scalar.copy, dst[:, 64:128, :], src[:, :, 64:128])
+        def weave_shared(dst, src):
+            weave(nc.vector.tensor_copy, dst[:, 0:VECTOR_SHARE, :], src[:, :, 0:VECTOR_SHARE])
+            weave(nc.scalar.copy, dst[:, VECTOR_SHARE:HALF, :], src[:, :, VECTOR_SHARE:HALF])
 
-        def quantise(codes, scales, src, c):
-            a, b = CHUNKS[c]
+        def quantise(codes, scales, woven, h):
             nc.vector.quantize_mx(
-                out=codes[:, a:b].bitcast(FP8X4), scales=scales[:, a:b], in_=src[c][:].rearrange("p c t -> p (c t)")
+                out=codes[:, half(h)].bitcast(FP8X4), scales=scales[:, half(h)], in_=woven[:].rearrange("p c t -> p (c t)")
             )
 
-        def out_of(dst, src, scale):
-            nc.scalar.activation(dst, src, COPY, scale=scale)
+        for t in (0, 1):
+            leave_psum(looked_up[t][:, half(0)], h_sums[t, 0], gain16[:, t : t + 1])
+            nc.vector.tensor_scalar_mul(plain[t][:, half(0)], h_sums[t, 0], gain16[:, t : t + 1])
+        for t in (0, 1):
+            leave_psum(looked_up[t][:, half(1)], h_sums[t, 1], gain16[:, t : t + 1])
+            leave_psum(plain[t][:, half(1)], h_sums[t, 1], gain16[:, t : t + 1])
+        for h in (0, 1):
+            difference(0, half(h))
+        difference(1, whole)
+        for t in (2, 3):
+            tanh(t - 2, 0)
+            z_values(t - 2, 0)
+            leave_psum(looked_up[t], h_sums[t], gain16[:, t : t + 1])
+            leave_psum(plain[t], h_sums[t], gain16[:, t : t + 1])
+            difference(t, whole)
+        for t in (2, 3):
+            tanh(t, 0)
+            z_values(t, 0)
+
+        for t in range(PACK - 1):
+            tanh(t, 1)
+            z_values(t, 1)
+        weave(nc.scalar.copy, z_bf16[0][:], z_f32[0][:])
+        quantise(z_codes, z_bytes, z_bf16[0], 0)
+        h2_first_half = [product(t, z_codes, z_bytes, half(0)) for t in (0, 1)]
+        tanh(PACK - 1, 1)
+        z_values(PACK - 1, 1)
 
         for t in (0, 1):
-            out_of(hw[t][:, half(0)], acc[t, 0], gain16[:, t : t + 1])
-            nc.vector.tensor_scalar_mul(hp[t][:, half(0)], acc[t, 0], gain16[:, t : t + 1])
+            leave_psum(looked_up[t][:, half(0)], h2_first_half[t], SIXTEENTH)
+        weave_shared(z_bf16[1], z_f32[1])
+        quantise(z_codes, z_bytes, z_bf16[1], 1)
         for t in (0, 1):
-            out_of(hw[t][:, half(1)], acc[t, 1], gain16[:, t : t + 1])
-            out_of(hp[t][:, half(1)], acc[t, 1], gain16[:, t : t + 1])
-        sub1(0, 0, HALF)
-        sub1(0, HALF, S)
-        sub1(1, 0, S)
-        for t in (2, 3):
-            tanh(t - 2, 0, HALF)
-            mul2(t - 2, 0)
-            out_of(hw[t], acc[t], gain16[:, t : t + 1])
-            out_of(hp[t], acc[t], gain16[:, t : t + 1])
-            sub1(t, 0, S)
-        for t in (2, 3):
-            tanh(t, 0, HALF)
-            mul2(t, 0)
-        for t in range(PACK):
-            tanh(t, HALF, S if t < 2 else CHUNKS[1][1])
-            mul2(t, 1)
-        for t in (0, 1):
-            mul2(t, 2)
-        h2 = [sb([P, S], F32, "h2_%d" % t) for t in range(PACK)]
+            leave_psum(looked_up[t][:, half(1)], product(t, z_codes, z_bytes, half(1)), SIXTEENTH)
+        h2_whole = {t: product(t, z_codes, z_bytes, whole) for t in (2, 3)}
+        leave_psum(looked_up[2][:, half(0)], h2_whole[2][:, half(0)], SIXTEENTH)
+        leave_psum(looked_up[3], h2_whole[3], SIXTEENTH)
+        leave_psum(looked_up[2][:, half(1)], h2_whole[2][:, half(1)], SIXTEENTH)
 
-        def second(t, a, b):
-            dst = bank()[:, 0 : b - a]
-            product(dst, t, z_codes, z_bytes, a, b)
-            return dst
+        at_n4 = [sbuf([P, S], F32, "at_n4_%d" % t) for t in range(PACK)]
+        out_f32 = [sbuf([P, PACK, HALF], F32, "out_f32_%d" % h) for h in (0, 1)]
+        out_bf16 = [sbuf([P, HALF, PACK], BF16, "out_bf16_%d" % h) for h in (0, 1)]
+        out_codes = sbuf([P, S], U32, "out_codes")
+        out_bytes = sbuf([P, S], U8, "out_bytes")
+        rows_0 = out_0.rearrange("(p t) j -> p t j", t=PACK)
+        words_1 = out_1[0].rearrange("p c t -> p (c t)").bitcast(I32)
+        pairs = ((0, 1), (2, 3))
 
-        weave(nc.scalar.copy, zb[0][:], zf[0][:])
-        quantise(z_codes, z_bytes, zb, 0)
-        early = [second(t, 0, HALF) for t in range(PACK)]
-        for t in (2, 3):
-            tanh(t, *CHUNKS[2])
-            mul2(t, 2)
-        weave(nc.scalar.copy, zb[1][:], zf[1][:])
-        out_of(h2[0][:, 0:HALF], early[0], SIXTEENTH)
-        weave_last(zb[2], zf[2])
-        for c in (1, 2):
-            quantise(z_codes, z_bytes, zb, c)
-            a, b = CHUNKS[c]
-            out_of(h2[0][:, a:b], second(0, a, b), SIXTEENTH)
-        late = [None] + [second(t, HALF, S) for t in range(1, PACK)]
+        def out_values(t, h):
+            nc.vector.tensor_tensor(
+                out_f32[h][:, t, :], window[t][:].indirect(entries(lists["n3"], half(h))), at_n4[t][:, half(h)], ALU.subtract
+            )
 
-        g4 = [sb([P, S], F32, "g4_%d" % t) for t in range(PACK)]
-        of = [sb([P, PACK, b - a], F32, "of%d" % a) for a, b in CHUNKS]
-        ob = [sb([P, b - a, PACK], BF16, "ob%d" % a) for a, b in CHUNKS]
-        o_codes = sb([P, S], U32, "o_codes")
-        o_bytes = sb([P, S], U8, "o_bytes")
-        out_rows = out_0.rearrange("(p t) j -> p t j", t=PACK)
-        out_codes = out_1[0].rearrange("p c t -> p (c t)").bitcast(I32)
-
-        def sub3(t, c):
-            a, b = CHUNKS[c]
-            nc.vector.tensor_tensor(of[c][:, t, :], h2[t][:].indirect(entries(lists["n3"], a, b)), g4[t][:, a:b], SUB)
-
-        for t in range(PACK):
-            if t > 0:
-                out_of(h2[t][:, half(0)], early[t], SIXTEENTH)
-                out_of(h2[t][:, half(1)], late[t], SIXTEENTH)
-            for h in (0, 1):
-                nc.vector.tensor_copy(g4[t][:, half(h)], h2[t][:].indirect(entries(lists["n4"], h * HALF, (h + 1) * HALF)))
-            if t > 0:
-                sub3(t - 1, 0)
-        sub3(PACK - 1, 0)
-        for c, (a, b) in enumerate(CHUNKS):
-            nc.sync.dma_start(out_rows[:, :, a:b], of[c][:])
-            if c < 2:
-                weave(nc.scalar.copy, ob[c][:], of[c][:])
-                for t in range(PACK):
-                    sub3(t, c + 1)
-            else:
-                weave_last(ob[c], of[c])
-        for c, (a, b) in enumerate(CHUNKS):
-            quantise(o_codes, o_bytes, ob, c)
-            nc.sync.dma_start(out_codes[:, a:b], o_codes[:].bitcast(I32)[:, a:b])
+        for pair in pairs:
+            for t in pair:
+                nc.vector.tensor_copy(at_n4[t][:], window[t][:].indirect(lists["n4"][:]))
+            for t in pair:
+                out_values(t, 0)
+        nc.sync.dma_start(rows_0[:, :, half(0)], out_f32[0][:])
+        weave(nc.scalar.copy, out_bf16[0][:], out_f32[0][:])
+        for pair in pairs:
+            for t in pair:
+                out_values(t, 1)
+            tiles = slice(pair[0], pair[1] + 1)
+            nc.sync.dma_start(rows_0[:, tiles, half(1)], out_f32[1][:, tiles, :])
+        weave_shared(out_bf16[1], out_f32[1])
+        for h in (0, 1):
+            quantise(out_codes, out_bytes, out_bf16[h], h)
+            nc.sync.dma_start(words_1[:, half(h)], out_codes[:].bitcast(I32)[:, half(h)])
         for q in range(4):
             queue = nc.sync if q < 2 else nc.scalar
-            queue.dma_start(out_2[0].bitcast(I32)[4 * q : 4 * q + 4, :], o_bytes[:].bitcast(I32)[32 * q : 32 * q + 4, :])
+            queue.dma_start(
+                out_2[0].bitcast(I32)[4 * q : 4 * q + 4, :], out_bytes[:].bitcast(I32)[QUADRANT * q : QUADRANT * q + 4, :]
+            )

from contextlib import ExitStack

import concourse.mybir as mybir

F32 = mybir.dt.float32
BF16 = mybir.dt.bfloat16
I32 = mybir.dt.int32
U32 = mybir.dt.uint32
U16 = mybir.dt.uint16
U8 = mybir.dt.uint8
FP8X4 = mybir.dt.float8_e4m3fn_x4
ALU = mybir.AluOpType
COPY = mybir.ActivationFunctionType.Copy
TANH = mybir.ActivationFunctionType.Tanh

P = 128
PACK = 4
QUADRANT = 32
SCALE_ROWS = 16
REPEAT = P // SCALE_ROWS
GROUP = 16
TABLE = 2048
S = 512
HALF = S // 2
SIXTEENTH = 0.0625
LARGEST = 2.0**127
VECTOR_SHARE = 160
BANKS = 8
FLOPS = 2 * 2 * 512 * 512 * 512


def half(h):
    return slice(h * HALF, (h + 1) * HALF)


def entries(offsets, cols):
    return offsets[:, cols.start // GROUP : cols.stop // GROUP]


def tile_picked_ringfdifgap_none_po_kernel(
    tc, x_words, x_scales, d_words, d_scales, gs, offs, k1, n1, n2, n3, n4, out_0, out_1, out_2
):
    nc = tc.nc
    whole = slice(0, S)
    with ExitStack() as ctx:
        keep = ctx.enter_context(tc.tile_pool(name="keep", bufs=1))
        psum = ctx.enter_context(tc.psum_pool(name="psum", bufs=BANKS))

        def sbuf(shape, dtype, name, tag=None):
            return keep.tile(shape, dtype, name=name, tag=tag or name, align_bytes=64)

        lists = {}

        def load_list(name, source):
            lists[name] = keep.tile([P, S // GROUP], U16, name="list_" + name)
            nc.sync.dma_start(lists[name][:], source)

        d_byte_table = sbuf([P, TABLE], U8, "d_byte_table")
        x_byte_table = sbuf([P, TABLE], U8, "x_byte_table")
        d_word_table = sbuf([P, TABLE], I32, "d_word_table")
        x_word_table = sbuf([P, TABLE], I32, "x_word_table")
        load_list("k1", k1)
        gain = sbuf([P, PACK], F32, "gain")
        nc.gpsimd.dma_start(gain[:], gs.rearrange("(p t) o -> p (t o)", t=PACK))
        nc.sync.dma_start(
            d_byte_table[:].bitcast(I32),
            d_scales[0].bitcast(I32).unsqueeze(1).broadcast_to([SCALE_ROWS, REPEAT, TABLE // 4]),
        )
        load_list("offs", offs)
        for q in (0, 2, 1, 3):
            nc.sync.dma_start(
                x_byte_table[:].bitcast(I32)[QUADRANT * q : QUADRANT * (q + 1), :],
                x_scales[0].bitcast(I32)[4 * q : 4 * q + 4, :].unsqueeze(0).broadcast_to([REPEAT, 4, TABLE // 4]),
            )
        nc.sync.dma_start(d_word_table[:], d_words[0].rearrange("p n t -> p (n t)").bitcast(I32))
        nc.sync.dma_start(x_word_table[:], x_words[0].rearrange("p n t -> p (n t)").bitcast(I32))
        for name, source in (("n1", n1), ("n2", n2), ("n3", n3), ("n4", n4)):
            load_list(name, source)

        gain16 = sbuf([P, PACK], F32, "gain16")
        nc.scalar.activation(gain16[:], gain[:], COPY, scale=SIXTEENTH)

        d_bytes_picked = sbuf([P, S], U8, "d_bytes_picked")
        nc.vector.tensor_copy(d_bytes_picked[:], d_byte_table[:].indirect(lists["k1"][:]))
        d_bytes = sbuf([P, S], U8, "d_bytes")
        nc.vector.tensor_copy(
            d_bytes[:].rearrange("p (t m) -> p t m", t=PACK), d_bytes_picked[:].rearrange("p (m t) -> p t m", t=PACK)
        )
        for r in range(1, 4):
            nc.scalar.dma_start(
                d_bytes[:].bitcast(I32)[r:P:QUADRANT, :], d_bytes[:].bitcast(I32)[REPEAT * r : P : QUADRANT, :]
            )

        x_bytes = sbuf([P, S], U8, "x_bytes")
        nc.vector.tensor_copy(x_bytes[:], x_byte_table[:].indirect(lists["offs"][:]))

        d_words_picked = sbuf([P, S], U32, "d_words_picked")
        nc.vector.tensor_copy(d_words_picked[:], d_word_table[:].bitcast(U32).indirect(lists["k1"][:]))
        d_codes = sbuf([P, S], U32, "d_codes")
        nc.vector.tensor_copy(
            d_codes[:].rearrange("p (t m i) -> p m t i", t=PACK, i=4),
            d_words_picked[:].rearrange("p (m i t) -> p m t i", t=PACK, i=4),
        )

        def product(t, codes, scales, cols):
            bank = psum.tile([P, S], F32, name="bank")
            sums = bank[:, 0 : cols.stop - cols.start]
            nc.tensor.matmul_mx(
                out=sums,
                lhsT=d_codes[:, t * P : (t + 1) * P].bitcast(FP8X4),
                lhsT_scale=d_bytes[:, t * P : (t + 1) * P],
                rhs=codes[:, cols].bitcast(FP8X4),
                rhs_scale=scales[:, cols],
                start=True,
                stop=True,
            )
            return sums

        x_codes = sbuf([P, S], U32, "x_codes")
        h_sums = {}
        for h in (0, 1):
            nc.vector.tensor_copy(
                x_codes[:, half(h)], x_word_table[:].bitcast(U32).indirect(entries(lists["offs"], half(h)))
            )
            for t in (0, 1):
                h_sums[t, h] = product(t, x_codes, x_bytes, half(h))
        inverse = sbuf([P, PACK], F32, "inverse", tag="x_word_table")
        nc.vector.reciprocal(inverse[:], gain[:])
        ungain = sbuf([P, PACK], F32, "ungain")
        nc.vector.tensor_scalar(ungain[:], inverse[:], LARGEST, -LARGEST, ALU.min, ALU.max)
        for t in (2, 3):
            h_sums[t] = product(t, x_codes, x_bytes, whole)

        window = [sbuf([P, 2 * S], F32, "window%d" % t) for t in range(PACK)]
        nc.vector.memset(window[0][:, S : 2 * S], 0.0)
        plain_last = sbuf([P, S], F32, "plain_last")
        looked_up = [w[:, 0:S] for w in window]
        plain = [w[:, S : 2 * S] for w in window[1:]] + [plain_last[:]]
        diff = [sbuf([P, S], F32, "diff%d" % t) for t in range(PACK)]
        tanh_diff = [sbuf([P, S], F32, "tanh_diff%d" % t) for t in range(PACK)]
        z_f32 = [sbuf([P, PACK, HALF], F32, "z_f32_%d" % h) for h in (0, 1)]
        z_bf16 = [sbuf([P, HALF, PACK], BF16, "z_bf16_%d" % h) for h in (0, 1)]
        z_codes = sbuf([P, S], U32, "z_codes")
        z_bytes = sbuf([P, S], U8, "z_bytes")

        def leave_psum(dst, sums, scale):
            nc.scalar.activation(dst, sums, COPY, scale=scale)

        def difference(t, cols):
            nc.vector.tensor_tensor(
                diff[t][:, cols], window[t][:].indirect(entries(lists["n1"], cols)), plain[t][:, cols], ALU.subtract
            )

        def tanh(t, h):
            nc.scalar.activation(tanh_diff[t][:, half(h)], diff[t][:, half(h)], TANH, scale=ungain[:, t : t + 1])

        def z_values(t, h):
            nc.vector.tensor_tensor(
                z_f32[h][:, t, :], window[t][:].indirect(entries(lists["n2"], half(h))), tanh_diff[t][:, half(h)], ALU.mult
            )

        def weave(copy, dst, src):
            copy(dst.rearrange("p (c i) t -> p c t i", i=2), src.rearrange("p t (c i) -> p c t i", i=2))

        def weave_shared(dst, src):
            weave(nc.vector.tensor_copy, dst[:, 0:VECTOR_SHARE, :], src[:, :, 0:VECTOR_SHARE])
            weave(nc.scalar.copy, dst[:, VECTOR_SHARE:HALF, :], src[:, :, VECTOR_SHARE:HALF])

        def quantise(codes, scales, woven, h):
            nc.vector.quantize_mx(
                out=codes[:, half(h)].bitcast(FP8X4), scales=scales[:, half(h)], in_=woven[:].rearrange("p c t -> p (c t)")
            )

        for t in (0, 1):
            leave_psum(looked_up[t][:, half(0)], h_sums[t, 0], gain16[:, t : t + 1])
            nc.vector.tensor_scalar_mul(plain[t][:, half(0)], h_sums[t, 0], gain16[:, t : t + 1])
        for t in (0, 1):
            leave_psum(looked_up[t][:, half(1)], h_sums[t, 1], gain16[:, t : t + 1])
            leave_psum(plain[t][:, half(1)], h_sums[t, 1], gain16[:, t : t + 1])
        for h in (0, 1):
            difference(0, half(h))
        difference(1, whole)
        for t in (2, 3):
            tanh(t - 2, 0)
            z_values(t - 2, 0)
            leave_psum(looked_up[t], h_sums[t], gain16[:, t : t + 1])
            leave_psum(plain[t], h_sums[t], gain16[:, t : t + 1])
            difference(t, whole)
        for t in (2, 3):
            tanh(t, 0)
            z_values(t, 0)

        for t in range(PACK - 1):
            tanh(t, 1)
            z_values(t, 1)
        weave(nc.scalar.copy, z_bf16[0][:], z_f32[0][:])
        quantise(z_codes, z_bytes, z_bf16[0], 0)
        h2_first_half = [product(t, z_codes, z_bytes, half(0)) for t in (0, 1)]
        tanh(PACK - 1, 1)
        z_values(PACK - 1, 1)

        for t in (0, 1):
            leave_psum(looked_up[t][:, half(0)], h2_first_half[t], SIXTEENTH)
        weave_shared(z_bf16[1], z_f32[1])
        quantise(z_codes, z_bytes, z_bf16[1], 1)
        for t in (0, 1):
            leave_psum(looked_up[t][:, half(1)], product(t, z_codes, z_bytes, half(1)), SIXTEENTH)
        h2_whole = {t: product(t, z_codes, z_bytes, whole) for t in (2, 3)}
        leave_psum(looked_up[2][:, half(0)], h2_whole[2][:, half(0)], SIXTEENTH)
        leave_psum(looked_up[3], h2_whole[3], SIXTEENTH)
        leave_psum(looked_up[2][:, half(1)], h2_whole[2][:, half(1)], SIXTEENTH)

        at_n4 = [sbuf([P, S], F32, "at_n4_%d" % t) for t in range(PACK)]
        out_f32 = [sbuf([P, PACK, HALF], F32, "out_f32_%d" % h) for h in (0, 1)]
        out_bf16 = [sbuf([P, HALF, PACK], BF16, "out_bf16_%d" % h) for h in (0, 1)]
        out_codes = sbuf([P, S], U32, "out_codes")
        out_bytes = sbuf([P, S], U8, "out_bytes")
        rows_0 = out_0.rearrange("(p t) j -> p t j", t=PACK)
        words_1 = out_1[0].rearrange("p c t -> p (c t)").bitcast(I32)
        pairs = ((0, 1), (2, 3))

        def out_values(t, h):
            nc.vector.tensor_tensor(
                out_f32[h][:, t, :], window[t][:].indirect(entries(lists["n3"], half(h))), at_n4[t][:, half(h)], ALU.subtract
            )

        for pair in pairs:
            for t in pair:
                nc.vector.tensor_copy(at_n4[t][:], window[t][:].indirect(lists["n4"][:]))
            for t in pair:
                out_values(t, 0)
        nc.sync.dma_start(rows_0[:, :, half(0)], out_f32[0][:])
        weave(nc.scalar.copy, out_bf16[0][:], out_f32[0][:])
        for pair in pairs:
            for t in pair:
                out_values(t, 1)
            tiles = slice(pair[0], pair[1] + 1)
            nc.sync.dma_start(rows_0[:, tiles, half(1)], out_f32[1][:, tiles, :])
        weave_shared(out_bf16[1], out_f32[1])
        for h in (0, 1):
            quantise(out_codes, out_bytes, out_bf16[h], h)
            nc.sync.dma_start(words_1[:, half(h)], out_codes[:].bitcast(I32)[:, half(h)])
        for q in range(4):
            queue = nc.sync if q < 2 else nc.scalar
            queue.dma_start(
                out_2[0].bitcast(I32)[4 * q : 4 * q + 4, :], out_bytes[:].bitcast(I32)[QUADRANT * q : QUADRANT * q + 4, :]
            )
